import numpy as np
import ml_dtypes


def mxq(x, axis, fmt="e4m3"):
    dtype, down = {"e4m3": (ml_dtypes.float8_e4m3fn, 7), "e5m2": (ml_dtypes.float8_e5m2, 14)}[fmt]
    v = np.moveaxis(np.asarray(x, np.float32).astype(ml_dtypes.bfloat16).astype(np.float64), axis, -1)
    blocks = v.reshape(v.shape[:-1] + (-1, 32))
    amax = np.abs(blocks).max(-1, keepdims=True)
    byte = np.maximum(np.where(amax > 0, np.frexp(amax)[1] - 1 + 127, 0) - down, 1)
    scale = np.exp2(byte - 127.0)
    codes = (blocks / scale).astype(np.float32).astype(dtype).astype(np.float64)
    return np.moveaxis((codes * scale).reshape(v.shape), -1, axis)


WIDE = False


def mx_kscale(k):
    if not WIDE:
        return np.ones(k)
    levels = np.array([30, -30])
    if k % 512:
        return np.exp2(np.random.permutation(np.resize(levels, k // 32))).repeat(32)
    a = np.empty((k // 512, 16))
    for p in range(k // 512):
        a[p, :8] = np.random.permutation(np.resize(levels, 8))
        for g in range(8):
            far = levels[np.abs(levels - a[p, g]) >= 10]
            a[p, g + 8] = far[np.random.randint(len(far))]
    return np.exp2(a.ravel()).repeat(32)


def f64(x):
    return np.asarray(x).astype(np.float64)


def striped(idx):
    return np.tile(np.asarray(idx).reshape(-1, 16).T, (8, 1)).astype(np.uint16)


def unstriped(offs):
    return offs[:16].T.reshape(-1).astype(np.int64)


E2M1 = np.array([0.0, 0.5, 1.0, 1.5, 2.0, 3.0, 4.0, 6.0, -0.0, -0.5, -1.0, -1.5, -2.0, -3.0, -4.0, -6.0])


def pack_weight(w, fmt):
    k, n = w.shape
    w = f64(np.asarray(w, np.float32).astype(ml_dtypes.bfloat16)).reshape(k // 32, 32, n)
    amax = np.abs(w).max(1)
    if fmt in ("e4m3", "e5m2"):
        byte = np.frexp(amax)[1] - 1 + 127 - (7 if fmt == "e4m3" else 14)
    else:
        mant, ex = np.frexp(amax / 6.0)
        byte = np.where(mant > 0.5, ex, ex - 1) + 127
    byte = np.clip(np.where(amax > 0, byte, 1), 1, 254)
    scaled = (w * np.exp2(127.0 - byte)[:, None, :]).reshape(k, n).astype(np.float32)
    by_word = np.ascontiguousarray(scaled.reshape(k // 512, 128, 4, n).transpose(0, 1, 3, 2))
    if fmt in ("e4m3", "e5m2"):
        words = by_word.astype(ml_dtypes.float8_e4m3fn if fmt == "e4m3" else ml_dtypes.float8_e5m2).view(np.uint8)
    else:
        c = by_word.astype(ml_dtypes.float4_e2m1fn).view(np.uint8) & 0xF
        words = (c[..., 0::2] | (c[..., 1::2] << 4)).reshape(k // 512, 128, 2 * n)
    return np.ascontiguousarray(words), np.ascontiguousarray(byte.astype(np.uint8).reshape(k // 512, 16, n))


def unpack_weight(words, scales, fmt):
    g, _, n = scales.shape
    words = np.ascontiguousarray(words).reshape(g, 128, n, -1)
    if fmt in ("e4m3", "e5m2"):
        vals = words.view(ml_dtypes.float8_e4m3fn if fmt == "e4m3" else ml_dtypes.float8_e5m2).astype(np.float64)
    else:
        nib = np.empty((g, 128, n, 4), np.uint8)
        nib[..., 0::2] = words & 0xF
        nib[..., 1::2] = words >> 4
        vals = E2M1[nib]
    vals = vals * np.repeat(np.exp2(scales.astype(np.float64) - 127.0), 8, axis=1)[..., None]
    return vals.transpose(0, 1, 3, 2).reshape(g * 512, n)


K, T, J, R, O, N, E = 512, 2048, 256, 512, 128, 256, 1024


def setup_inputs():
    n = np.random.standard_normal
    idx = np.random.permutation(T)[:J]
    idx2 = np.random.permutation(T)[:J]
    idx3 = np.random.permutation(J)[:O]
    idx4 = np.random.permutation(J)[:O]
    idx5 = np.random.permutation(E)[:O]
    fk = mx_kscale(K)
    fr = mx_kscale(R)
    xtp = pack_weight(n((K, T)) / fk[:, None], "e4m3")
    wp = pack_weight(n((K, R)) * 1 / np.sqrt(K) * fk[:, None] * fr, "e2m1")
    w2p = pack_weight(n((K, R)) * 1 / np.sqrt(K) * fk[:, None] * fr, "e5m2")
    wbp = pack_weight(n((R, N)) * 1 / np.sqrt(R) / fr[:, None], "e5m2")
    return {
        "xt_words": xtp[0],
        "xt_scales": xtp[1],
        "w_words": wp[0],
        "w_scales": wp[1],
        "w2_words": w2p[0],
        "w2_scales": w2p[1],
        "wb_words": wbp[0],
        "wb_scales": wbp[1],
        "offs": striped(idx),
        "offs2": striped(idx2),
        "offs3": striped(idx3),
        "offs4": striped(idx4),
        "offs5": striped(idx5),
    }


def reference(xt_words, xt_scales, w_words, w_scales, w2_words, w2_scales, wb_words, wb_scales, offs, offs2, offs3, offs4, offs5):
    idx = unstriped(offs)
    idx2 = unstriped(offs2)
    idx3 = unstriped(offs3)
    idx4 = unstriped(offs4)
    idx5 = unstriped(offs5)
    xtu = unpack_weight(xt_words, xt_scales, "e4m3")
    wu = unpack_weight(w_words, w_scales, "e2m1")
    w2u = unpack_weight(w2_words, w2_scales, "e5m2")
    wbu = unpack_weight(wb_words, wb_scales, "e5m2")
    xtidxg = xtu[:, idx]
    a = wu.T @ xtidxg
    xtidx2g = xtu[:, idx2]
    b = w2u.T @ xtidx2g
    hid = np.maximum(a[:, idx3], b[:, idx4])
    hidq = mxq(hid, 0, "e4m3")
    p = wbu.T @ hidq
    y = np.zeros((N, E))
    y[:, idx5] = p
    return y

@@ -1,0 +1,153 @@
+from contextlib import ExitStack
+
+import concourse.mybir as mybir
+
+K, T, J, R, O, N, E = 512, 2048, 256, 512, 128, 256, 1024
+FLOPS = 2 * K * R * J * 2 + 2 * R * N * O
+
+F32 = mybir.dt.float32
+BF16 = mybir.dt.bfloat16
+I32 = mybir.dt.int32
+U32 = mybir.dt.uint32
+U16 = mybir.dt.uint16
+U8 = mybir.dt.uint8
+E4M3 = mybir.dt.float8_e4m3fn_x4
+E5M2 = mybir.dt.float8_e5m2_x4
+E2M1 = mybir.dt.float4_e2m1fn_x4
+COPY = mybir.ActivationFunctionType.Copy
+MAX = mybir.AluOpType.max
+
+P = 128
+PACK = 4
+
+
+def tile_list_ahead_looked_one_scattered_kernel(
+    tc, xt_words, xt_scales, w_words, w_scales, w2_words, w2_scales, wb_words, wb_scales,
+    offs, offs2, offs3, offs4, offs5, out,
+):
+    nc = tc.nc
+    with ExitStack() as ctx:
+        sb = ctx.enter_context(tc.tile_pool(name="sb", bufs=1))
+        ps = ctx.enter_context(tc.psum_pool(name="ps", bufs=1))
+
+        def tile(name, cols, dtype):
+            return sb.tile([P, cols], dtype, name=name, align_bytes=64)
+
+        def load_list(name, src):
+            lst = tile(name, src.shape[1], U16)
+            nc.sync.dma_start(lst[:], src)
+            return lst
+
+        def load_words(name, src, cols, dtype):
+            words = tile(name, cols, dtype)
+            nc.sync.dma_start(words[:].bitcast(I32), src.bitcast(I32))
+            return words
+
+        def zeroed_plane(engine, name, cols):
+            plane = tile(name, cols, U8)
+            engine.memset(plane[:].bitcast(I32), 0)
+            return plane
+
+        def load_scales(queue, plane, src):
+            for q in range(4):
+                queue.dma_start(plane[32 * q : 32 * q + 4, :].bitcast(I32), src[0, 4 * q : 4 * q + 4, :].bitcast(I32))
+
+        def deal_columns(name, src, dtype, run):
+            dst = tile(name, R, dtype)
+            nc.vector.tensor_copy(
+                dst[:].rearrange("p (t c i) -> p c t i", t=PACK, i=run),
+                src[:].rearrange("p (c i t) -> p c t i", t=PACK, i=run),
+            )
+            return dst
+
+        def flat(words):
+            return words[0].rearrange("p n t -> p (n t)")
+
+        xs = tile("xs", T, U8)
+        nc.vector.memset(xs[:, : T // 2].bitcast(I32), 0)
+        nc.gpsimd.memset(xs[:, T // 2 :].bitcast(I32), 0)
+        w2s_raw = zeroed_plane(nc.gpsimd, "w2s_raw", R)
+        list1 = load_list("list1", offs)
+        list2 = load_list("list2", offs2)
+        ww_raw = load_words("ww_raw", w_words[0], R, U16)
+        load_scales(nc.sync, xs, xt_scales)
+        xw = load_words("xw", flat(xt_words), T, U32)
+        load_scales(nc.gpsimd, w2s_raw, w2_scales)
+
+        pages = []
+        for h in range(N // P):
+            page = tile("page%d" % h, E, F32)
+            nc.vector.memset(page[:], 0.0)
+            pages.append(page)
+        ws_raw = zeroed_plane(nc.vector, "ws_raw", R)
+        load_scales(nc.scalar, ws_raw, w_scales)
+        w2w_raw = load_words("w2w_raw", flat(w2_words), R, U32)
+        list3 = load_list("list3", offs3)
+        list4 = load_list("list4", offs4)
+        list5 = load_list("list5", offs5)
+
+        def gather(name, window, lst, cols, dtype):
+            picked = tile(name, cols, dtype)
+            nc.vector.tensor_copy(picked[:], window[:].indirect(lst[:]))
+            return picked
+
+        x1s = gather("x1s", xs, list1, J, U8)
+        ww = deal_columns("ww", ww_raw, U16, 8)
+        x2s = gather("x2s", xs, list2, J, U8)
+        ws = deal_columns("ws", ws_raw, U8, 16)
+        wbw = load_words("ww_raw", flat(wb_words), N, U32)
+        wbs = ws_raw[:, 0:N]
+        load_scales(nc.sync, wbs, wb_scales)
+        x1w = gather("x1w", xw, list1, J, U32)
+        x2w = gather("x2w", xw, list2, J, U32)
+        w2s = deal_columns("xw", w2s_raw, U8, 16)
+        w2w = deal_columns("w2w", w2w_raw, U32, 4)
+
+        def vector_copy(dst, src):
+            nc.vector.tensor_copy(dst, src)
+
+        def scalar_copy(dst, src):
+            nc.scalar.activation(dst, src, COPY)
+
+        picked_a = tile("picked_a", PACK * O, F32)
+        picked_b = tile("picked_b", PACK * O, F32)
+
+        def first_stage(name, t, words, scales, fmt, xwords, xscales, lst, picked, copy):
+            cols = slice(P * t, P * (t + 1))
+            acc = ps.tile([P, J], F32, name="acc_" + name, tag="bank_" + name)
+            nc.tensor.matmul_mx(
+                acc[:], lhsT=words[:, cols].bitcast(fmt), lhsT_scale=scales[:, cols],
+                rhs=xwords[:].bitcast(E4M3), rhs_scale=xscales[:], start=True, stop=True,
+            )
+            whole = tile("whole_" + name, J, F32)
+            copy(whole[:], acc[:])
+            copy(picked[:, O * t : O * (t + 1)], whole[:].indirect(lst[:]))
+
+        for t in range(PACK):
+            first_stage("a%d" % t, t, ww, ws, E2M1, x1w, x1s, list3, picked_a, scalar_copy)
+        for t in range(PACK):
+            copy = scalar_copy if t == PACK - 1 else vector_copy
+            first_stage("b%d" % t, t, w2w, w2s, E5M2, x2w, x2s, list4, picked_b, copy)
+
+        hid = tile("hid", PACK * O, BF16)
+        nc.vector.tensor_tensor(
+            hid[:].rearrange("p (c i t) -> p c t i", t=PACK, i=4),
+            picked_a[:].rearrange("p (t c i) -> p c t i", t=PACK, i=4),
+            picked_b[:].rearrange("p (t c i) -> p c t i", t=PACK, i=4),
+            MAX,
+        )
+        hw = tile("hw", O, U32)
+        hs = tile("hs", O, U8)
+        nc.vector.quantize_mx(hw[:].bitcast(E4M3), hs[:], hid[:])
+
+        for h, (copy, queue) in enumerate(((vector_copy, nc.sync), (scalar_copy, nc.scalar))):
+            cols = slice(P * h, P * (h + 1))
+            acc = ps.tile([P, O], F32, name="acc_p%d" % h, tag="bank_a%d" % h)
+            nc.tensor.matmul_mx(
+                acc[:], lhsT=wbw[:, cols].bitcast(E5M2), lhsT_scale=wbs[:, cols],
+                rhs=hw[:].bitcast(E4M3), rhs_scale=hs[:], start=True, stop=True,
+            )
+            rows = tile("rows%d" % h, O, F32)
+            copy(rows[:], acc[:])
+            copy(pages[h][:].indirect(list5[:]), rows[:])
+            queue.dma_start(out[cols, :], pages[h][:])

@@ -38,9 +38,9 @@ def tile_list_ahead_looked_one_scattered_kernel(
             nc.sync.dma_start(lst[:], src)
             return lst
 
-        def load_words(name, src, cols, dtype):
+        def load_words(queue, name, src, cols, dtype):
             words = tile(name, cols, dtype)
-            nc.sync.dma_start(words[:].bitcast(I32), src.bitcast(I32))
+            queue.dma_start(words[:].bitcast(I32), src.bitcast(I32))
             return words
 
         def zeroed_plane(engine, name, cols):
@@ -48,14 +48,13 @@ def tile_list_ahead_looked_one_scattered_kernel(
             engine.memset(plane[:].bitcast(I32), 0)
             return plane
 
-        def load_scales(queue, plane, src):
-            for q in range(4):
+        def load_scales(queues, plane, src):
+            for q, queue in enumerate(queues):
                 queue.dma_start(plane[32 * q : 32 * q + 4, :].bitcast(I32), src[0, 4 * q : 4 * q + 4, :].bitcast(I32))
 
-        def deal_columns(name, src, dtype, run):
-            dst = tile(name, R, dtype)
+        def deal_columns(dst, src, run):
             nc.vector.tensor_copy(
-                dst[:].rearrange("p (t c i) -> p c t i", t=PACK, i=run),
+                dst.rearrange("p (t c i) -> p c t i", t=PACK, i=run),
                 src[:].rearrange("p (c i t) -> p c t i", t=PACK, i=run),
             )
             return dst
@@ -63,28 +62,29 @@ def tile_list_ahead_looked_one_scattered_kernel(
         def flat(words):
             return words[0].rearrange("p n t -> p (n t)")
 
-        xs = tile("xs", T, U8)
-        nc.vector.memset(xs[:, : T // 2].bitcast(I32), 0)
-        nc.gpsimd.memset(xs[:, T // 2 :].bitcast(I32), 0)
+        xs = zeroed_plane(nc.vector, "xs", T)
         w2s_raw = zeroed_plane(nc.gpsimd, "w2s_raw", R)
-        list1 = load_list("list1", offs)
-        list2 = load_list("list2", offs2)
-        ww_raw = load_words("ww_raw", w_words[0], R, U16)
-        load_scales(nc.sync, xs, xt_scales)
-        xw = load_words("xw", flat(xt_words), T, U32)
-        load_scales(nc.gpsimd, w2s_raw, w2_scales)
-
         pages = []
         for h in range(N // P):
             page = tile("page%d" % h, E, F32)
             nc.vector.memset(page[:], 0.0)
             pages.append(page)
+        wbs = zeroed_plane(nc.vector, "wbs", N)
         ws_raw = zeroed_plane(nc.vector, "ws_raw", R)
-        load_scales(nc.scalar, ws_raw, w_scales)
-        w2w_raw = load_words("w2w_raw", flat(w2_words), R, U32)
+
+        list1 = load_list("list1", offs)
+        list2 = load_list("list2", offs2)
+        load_scales([nc.sync] * 2 + [nc.scalar] * 2, xs, xt_scales)
+        ww_raw = load_words(nc.scalar, "ww_raw", w_words[0], R, U16)
+        xw = load_words(nc.sync, "xw", flat(xt_words), T, U32)
+        load_scales([nc.scalar] * 4, ws_raw, w_scales)
+        w2w_raw = load_words(nc.sync, "w2w_raw", flat(w2_words), R, U32)
         list3 = load_list("list3", offs3)
+        load_scales([nc.sync] + [nc.gpsimd] * 3, w2s_raw, w2_scales)
         list4 = load_list("list4", offs4)
         list5 = load_list("list5", offs5)
+        wbw = load_words(nc.sync, "wbw", flat(wb_words), N, U32)
+        load_scales([nc.sync] * 4, wbs, wb_scales)
 
         def gather(name, window, lst, cols, dtype):
             picked = tile(name, cols, dtype)
@@ -92,16 +92,14 @@ def tile_list_ahead_looked_one_scattered_kernel(
             return picked
 
         x1s = gather("x1s", xs, list1, J, U8)
-        ww = deal_columns("ww", ww_raw, U16, 8)
+        ww = deal_columns(tile("ww", R, U16)[:], ww_raw, 8)
         x2s = gather("x2s", xs, list2, J, U8)
-        ws = deal_columns("ws", ws_raw, U8, 16)
-        wbw = load_words("ww_raw", flat(wb_words), N, U32)
-        wbs = ws_raw[:, 0:N]
-        load_scales(nc.sync, wbs, wb_scales)
         x1w = gather("x1w", xw, list1, J, U32)
-        x2w = gather("x2w", xw, list2, J, U32)
-        w2s = deal_columns("xw", w2s_raw, U8, 16)
-        w2w = deal_columns("w2w", w2w_raw, U32, 4)
+        ws = deal_columns(tile("ws", R, U8)[:], ws_raw, 16)
+        x2w = gather("ws_raw", xw, list2, J, U32)
+        w2_dealt = tile("xw", 5 * R, U8)
+        w2w = deal_columns(w2_dealt[:, : 4 * R].bitcast(U32), w2w_raw, 4)
+        w2s = deal_columns(w2_dealt[:, 4 * R :], w2s_raw, 16)
 
         def vector_copy(dst, src):
             nc.vector.tensor_copy(dst, src)
@@ -112,22 +110,28 @@ def tile_list_ahead_looked_one_scattered_kernel(
         picked_a = tile("picked_a", PACK * O, F32)
         picked_b = tile("picked_b", PACK * O, F32)
 
-        def first_stage(name, t, words, scales, fmt, xwords, xscales, lst, picked, copy):
-            cols = slice(P * t, P * (t + 1))
-            acc = ps.tile([P, J], F32, name="acc_" + name, tag="bank_" + name)
-            nc.tensor.matmul_mx(
-                acc[:], lhsT=words[:, cols].bitcast(fmt), lhsT_scale=scales[:, cols],
-                rhs=xwords[:].bitcast(E4M3), rhs_scale=xscales[:], start=True, stop=True,
-            )
-            whole = tile("whole_" + name, J, F32)
-            copy(whole[:], acc[:])
-            copy(picked[:, O * t : O * (t + 1)], whole[:].indirect(lst[:]))
+        def first_stage(name, pair, words, scales, fmt, xwords, xscales):
+            acc = ps.tile([P, 2 * J], F32, name="acc_" + name, tag="bank_" + name)
+            for u in range(2):
+                cols = slice(P * (2 * pair + u), P * (2 * pair + u + 1))
+                nc.tensor.matmul_mx(
+                    acc[:, J * u : J * (u + 1)], lhsT=words[:, cols].bitcast(fmt), lhsT_scale=scales[:, cols],
+                    rhs=xwords[:].bitcast(E4M3), rhs_scale=xscales[:], start=True, stop=True,
+                )
+            whole = tile("whole_" + name, 2 * J, F32)
+            scalar_copy(whole[:], acc[:])
+            return whole
 
+        def pick(whole, t, lst, picked, copy):
+            u = t % 2
+            copy(picked[:, O * t : O * (t + 1)], whole[t // 2][:, J * u : J * (u + 1)].indirect(lst[:]))
+
+        a = [first_stage("a%d" % pair, pair, ww, ws, E2M1, x1w, x1s) for pair in range(2)]
+        b = [first_stage("b%d" % pair, pair, w2w, w2s, E5M2, x2w, x2s) for pair in range(2)]
         for t in range(PACK):
-            first_stage("a%d" % t, t, ww, ws, E2M1, x1w, x1s, list3, picked_a, scalar_copy)
+            pick(a, t, list3, picked_a, vector_copy)
         for t in range(PACK):
-            copy = scalar_copy if t == PACK - 1 else vector_copy
-            first_stage("b%d" % t, t, w2w, w2s, E5M2, x2w, x2s, list4, picked_b, copy)
+            pick(b, t, list4, picked_b, scalar_copy if t == PACK - 1 else vector_copy)
 
         hid = tile("hid", PACK * O, BF16)
         nc.vector.tensor_tensor(
@@ -142,7 +146,7 @@ def tile_list_ahead_looked_one_scattered_kernel(
 
         for h, (copy, queue) in enumerate(((vector_copy, nc.sync), (scalar_copy, nc.scalar))):
             cols = slice(P * h, P * (h + 1))
-            acc = ps.tile([P, O], F32, name="acc_p%d" % h, tag="bank_a%d" % h)
+            acc = ps.tile([P, O], F32, name="acc_p%d" % h, tag="bank_p%d" % h)
             nc.tensor.matmul_mx(
                 acc[:], lhsT=wbw[:, cols].bitcast(E5M2), lhsT_scale=wbs[:, cols],
                 rhs=hw[:].bitcast(E4M3), rhs_scale=hs[:], start=True, stop=True,

@@ -52,8 +52,8 @@ def tile_list_ahead_looked_one_scattered_kernel(
             for q, queue in enumerate(queues):
                 queue.dma_start(plane[32 * q : 32 * q + 4, :].bitcast(I32), src[0, 4 * q : 4 * q + 4, :].bitcast(I32))
 
-        def deal_columns(dst, src, run):
-            nc.vector.tensor_copy(
+        def deal_columns(move, dst, src, run):
+            move(
                 dst.rearrange("p (t c i) -> p c t i", t=PACK, i=run),
                 src[:].rearrange("p (c i t) -> p c t i", t=PACK, i=run),
             )
@@ -62,25 +62,27 @@ def tile_list_ahead_looked_one_scattered_kernel(
         def flat(words):
             return words[0].rearrange("p n t -> p (n t)")
 
-        xs = zeroed_plane(nc.vector, "xs", T)
-        w2s_raw = zeroed_plane(nc.gpsimd, "w2s_raw", R)
+        xs = tile("xs", T, U8)
+        nc.vector.memset(xs[:, : T // 2].bitcast(I32), 0)
+        nc.gpsimd.memset(xs[:, T // 2 :].bitcast(I32), 0)
+        ws_raw = zeroed_plane(nc.vector, "ws_raw", R)
+        w2s_raw = zeroed_plane(nc.vector, "w2s_raw", R)
+        wbs = zeroed_plane(nc.vector, "wbs", N)
         pages = []
         for h in range(N // P):
             page = tile("page%d" % h, E, F32)
             nc.vector.memset(page[:], 0.0)
             pages.append(page)
-        wbs = zeroed_plane(nc.vector, "wbs", N)
-        ws_raw = zeroed_plane(nc.vector, "ws_raw", R)
 
         list1 = load_list("list1", offs)
         list2 = load_list("list2", offs2)
-        load_scales([nc.sync] * 2 + [nc.scalar] * 2, xs, xt_scales)
         ww_raw = load_words(nc.scalar, "ww_raw", w_words[0], R, U16)
-        xw = load_words(nc.sync, "xw", flat(xt_words), T, U32)
-        load_scales([nc.scalar] * 4, ws_raw, w_scales)
-        w2w_raw = load_words(nc.sync, "w2w_raw", flat(w2_words), R, U32)
+        load_scales([nc.sync] * 2 + [nc.scalar] * 2, xs, xt_scales)
+        xw = load_words(nc.scalar, "xw", flat(xt_words), T, U32)
+        load_scales([nc.sync] * 4, ws_raw, w_scales)
+        w2w_raw = load_words(nc.scalar, "w2w_raw", flat(w2_words), R, U32)
+        load_scales([nc.sync] * 4, w2s_raw, w2_scales)
         list3 = load_list("list3", offs3)
-        load_scales([nc.sync] + [nc.gpsimd] * 3, w2s_raw, w2_scales)
         list4 = load_list("list4", offs4)
         list5 = load_list("list5", offs5)
         wbw = load_words(nc.sync, "wbw", flat(wb_words), N, U32)
@@ -92,14 +94,13 @@ def tile_list_ahead_looked_one_scattered_kernel(
             return picked
 
         x1s = gather("x1s", xs, list1, J, U8)
-        ww = deal_columns(tile("ww", R, U16)[:], ww_raw, 8)
+        ww = deal_columns(nc.vector.tensor_copy, tile("ww", R, U16)[:], ww_raw, 8)
         x2s = gather("x2s", xs, list2, J, U8)
         x1w = gather("x1w", xw, list1, J, U32)
-        ws = deal_columns(tile("ws", R, U8)[:], ws_raw, 16)
+        ws = deal_columns(nc.vector.tensor_copy, tile("ws", R, U8)[:], ws_raw, 16)
         x2w = gather("ws_raw", xw, list2, J, U32)
-        w2_dealt = tile("xw", 5 * R, U8)
-        w2w = deal_columns(w2_dealt[:, : 4 * R].bitcast(U32), w2w_raw, 4)
-        w2s = deal_columns(w2_dealt[:, 4 * R :], w2s_raw, 16)
+        w2w = deal_columns(nc.scalar.copy, tile("w2w", R, U32)[:], w2w_raw, 4)
+        w2s = deal_columns(nc.vector.tensor_copy, tile("xw", R, U8)[:], w2s_raw, 16)
 
         def vector_copy(dst, src):
             nc.vector.tensor_copy(dst, src)
@@ -107,10 +108,10 @@ def tile_list_ahead_looked_one_scattered_kernel(
         def scalar_copy(dst, src):
             nc.scalar.activation(dst, src, COPY)
 
-        picked_a = tile("picked_a", PACK * O, F32)
+        picked_a = tile("w2s_raw", PACK * O, F32)
         picked_b = tile("picked_b", PACK * O, F32)
 
-        def first_stage(name, pair, words, scales, fmt, xwords, xscales):
+        def first_stage(name, pair, words, scales, fmt, xwords, xscales, copy):
             acc = ps.tile([P, 2 * J], F32, name="acc_" + name, tag="bank_" + name)
             for u in range(2):
                 cols = slice(P * (2 * pair + u), P * (2 * pair + u + 1))
@@ -119,27 +120,28 @@ def tile_list_ahead_looked_one_scattered_kernel(
                     rhs=xwords[:].bitcast(E4M3), rhs_scale=xscales[:], start=True, stop=True,
                 )
             whole = tile("whole_" + name, 2 * J, F32)
-            scalar_copy(whole[:], acc[:])
+            copy(whole[:], acc[:])
             return whole
 
         def pick(whole, t, lst, picked, copy):
             u = t % 2
             copy(picked[:, O * t : O * (t + 1)], whole[t // 2][:, J * u : J * (u + 1)].indirect(lst[:]))
 
-        a = [first_stage("a%d" % pair, pair, ww, ws, E2M1, x1w, x1s) for pair in range(2)]
-        b = [first_stage("b%d" % pair, pair, w2w, w2s, E5M2, x2w, x2s) for pair in range(2)]
-        for t in range(PACK):
-            pick(a, t, list3, picked_a, vector_copy)
-        for t in range(PACK):
-            pick(b, t, list4, picked_b, scalar_copy if t == PACK - 1 else vector_copy)
-
+        copies = (vector_copy, scalar_copy)
+        a = [first_stage("a%d" % pair, pair, ww, ws, E2M1, x1w, x1s, scalar_copy) for pair in range(2)]
+        b = [first_stage("b%d" % pair, pair, w2w, w2s, E5M2, x2w, x2s, copies[pair]) for pair in range(2)]
         hid = tile("hid", PACK * O, BF16)
-        nc.vector.tensor_tensor(
-            hid[:].rearrange("p (c i t) -> p c t i", t=PACK, i=4),
-            picked_a[:].rearrange("p (t c i) -> p c t i", t=PACK, i=4),
-            picked_b[:].rearrange("p (t c i) -> p c t i", t=PACK, i=4),
-            MAX,
-        )
+        for pair in range(2):
+            for whole, lst, picked in ((a, list3, picked_a), (b, list4, picked_b)):
+                for t in (2 * pair, 2 * pair + 1):
+                    pick(whole, t, lst, picked, copies[pair])
+            slots = slice(2 * pair, 2 * pair + 2)
+            nc.vector.tensor_tensor(
+                hid[:].rearrange("p (c i t) -> p c t i", t=PACK, i=4)[:, :, slots, :],
+                picked_a[:].rearrange("p (t c i) -> p c t i", t=PACK, i=4)[:, :, slots, :],
+                picked_b[:].rearrange("p (t c i) -> p c t i", t=PACK, i=4)[:, :, slots, :],
+                MAX,
+            )
         hw = tile("hw", O, U32)
         hs = tile("hs", O, U8)
         nc.vector.quantize_mx(hw[:].bitcast(E4M3), hs[:], hid[:])

@@ -19,6 +19,8 @@ MAX = mybir.AluOpType.max
 
 P = 128
 PACK = 4
+QUAD = 32
+LINE = 16
 
 
 def tile_list_ahead_looked_one_scattered_kernel(
@@ -30,8 +32,8 @@ def tile_list_ahead_looked_one_scattered_kernel(
         sb = ctx.enter_context(tc.tile_pool(name="sb", bufs=1))
         ps = ctx.enter_context(tc.psum_pool(name="ps", bufs=1))
 
-        def tile(name, cols, dtype):
-            return sb.tile([P, cols], dtype, name=name, align_bytes=64)
+        def tile(buffer, cols, dtype):
+            return sb.tile([P, cols], dtype, name=buffer, align_bytes=64)
 
         def load_list(name, src):
             lst = tile(name, src.shape[1], U16)
@@ -43,31 +45,43 @@ def tile_list_ahead_looked_one_scattered_kernel(
             queue.dma_start(words[:].bitcast(I32), src.bitcast(I32))
             return words
 
-        def zeroed_plane(engine, name, cols):
+        def zeroed_plane(name, cols):
             plane = tile(name, cols, U8)
-            engine.memset(plane[:].bitcast(I32), 0)
+            nc.vector.memset(plane[:].bitcast(I32), 0)
             return plane
 
         def load_scales(queues, plane, src):
             for q, queue in enumerate(queues):
-                queue.dma_start(plane[32 * q : 32 * q + 4, :].bitcast(I32), src[0, 4 * q : 4 * q + 4, :].bitcast(I32))
+                queue.dma_start(
+                    plane[QUAD * q : QUAD * q + 4, :].bitcast(I32), src[0, 4 * q : 4 * q + 4, :].bitcast(I32)
+                )
 
-        def deal_columns(move, dst, src, run):
+        def deal_columns(move, dst, src, run, slices):
             move(
-                dst.rearrange("p (t c i) -> p c t i", t=PACK, i=run),
-                src[:].rearrange("p (c i t) -> p c t i", t=PACK, i=run),
+                dst[:].rearrange("p (t c i) -> p c t i", t=PACK, i=run)[:, :, slices, :],
+                src[:].rearrange("p (c i t) -> p c t i", t=PACK, i=run)[:, :, slices, :],
             )
-            return dst
+
+        def gather_packed(buffer, window, lst, dtype):
+            picked = tile(buffer, J, dtype)
+            nc.vector.tensor_copy(picked[:], window[:].indirect(lst[:]))
+            return picked
 
         def flat(words):
             return words[0].rearrange("p n t -> p (n t)")
 
-        xs = tile("xs", T, U8)
-        nc.vector.memset(xs[:, : T // 2].bitcast(I32), 0)
-        nc.gpsimd.memset(xs[:, T // 2 :].bitcast(I32), 0)
-        ws_raw = zeroed_plane(nc.vector, "ws_raw", R)
-        w2s_raw = zeroed_plane(nc.vector, "w2s_raw", R)
-        wbs = zeroed_plane(nc.vector, "wbs", N)
+        def vector_copy(dst, src):
+            nc.vector.tensor_copy(dst, src)
+
+        def scalar_copy(dst, src):
+            nc.scalar.activation(dst, src, COPY)
+
+        xt_plane = tile("xt_plane", T, U8)
+        nc.vector.memset(xt_plane[:, : T // 2].bitcast(I32), 0)
+        nc.gpsimd.memset(xt_plane[:, T // 2 :].bitcast(I32), 0)
+        w_plane_raw = zeroed_plane("w_plane_raw", R)
+        w2_plane_raw = zeroed_plane("w2_plane_raw", R)
+        wb_plane = zeroed_plane("wb_plane", N)
         pages = []
         for h in range(N // P):
             page = tile("page%d" % h, E, F32)
@@ -76,84 +90,80 @@ def tile_list_ahead_looked_one_scattered_kernel(
 
         list1 = load_list("list1", offs)
         list2 = load_list("list2", offs2)
-        ww_raw = load_words(nc.scalar, "ww_raw", w_words[0], R, U16)
-        load_scales([nc.sync] * 2 + [nc.scalar] * 2, xs, xt_scales)
-        xw = load_words(nc.scalar, "xw", flat(xt_words), T, U32)
-        load_scales([nc.sync] * 4, ws_raw, w_scales)
-        w2w_raw = load_words(nc.scalar, "w2w_raw", flat(w2_words), R, U32)
-        load_scales([nc.sync] * 4, w2s_raw, w2_scales)
+        w_raw = load_words(nc.scalar, "w_raw", w_words[0], R, U16)
+        load_scales([nc.sync] * 2 + [nc.scalar] * 2, xt_plane, xt_scales)
+        xt_table = load_words(nc.scalar, "xt_table", flat(xt_words), T, U32)
+        load_scales([nc.sync] * 4, w_plane_raw, w_scales)
+        w2_raw = load_words(nc.scalar, "w2_raw", flat(w2_words), R, U32)
+        load_scales([nc.sync] * 4, w2_plane_raw, w2_scales)
         list3 = load_list("list3", offs3)
         list4 = load_list("list4", offs4)
         list5 = load_list("list5", offs5)
-        wbw = load_words(nc.sync, "wbw", flat(wb_words), N, U32)
-        load_scales([nc.sync] * 4, wbs, wb_scales)
+        wb = load_words(nc.sync, "wb", flat(wb_words), N, U32)
+        load_scales([nc.sync] * 4, wb_plane, wb_scales)
 
-        def gather(name, window, lst, cols, dtype):
-            picked = tile(name, cols, dtype)
-            nc.vector.tensor_copy(picked[:], window[:].indirect(lst[:]))
-            return picked
+        every = slice(0, PACK)
+        pairs = [slice(0, 2), slice(2, 4)]
+        x1_plane = gather_packed("x1_plane", xt_plane, list1, U8)
+        w = tile("w", R, U16)
+        deal_columns(nc.vector.tensor_copy, w, w_raw, LINE // 2, every)
+        x2_plane = gather_packed("x2_plane", xt_plane, list2, U8)
+        x1 = gather_packed("x1", xt_table, list1, U32)
+        w_plane = tile("w_plane", R, U8)
+        for slices in pairs:
+            deal_columns(nc.vector.tensor_copy, w_plane, w_plane_raw, LINE, slices)
+        x2 = gather_packed("w_plane_raw", xt_table, list2, U32)
+        w2 = tile("w2", R, U32)
+        deal_columns(nc.scalar.copy, w2, w2_raw, LINE // 4, every)
+        w2_plane = tile("xt_table", R, U8)
+        deal_columns(nc.vector.tensor_copy, w2_plane, w2_plane_raw, LINE, every)
 
-        x1s = gather("x1s", xs, list1, J, U8)
-        ww = deal_columns(nc.vector.tensor_copy, tile("ww", R, U16)[:], ww_raw, 8)
-        x2s = gather("x2s", xs, list2, J, U8)
-        x1w = gather("x1w", xw, list1, J, U32)
-        ws = deal_columns(nc.vector.tensor_copy, tile("ws", R, U8)[:], ws_raw, 16)
-        x2w = gather("ws_raw", xw, list2, J, U32)
-        w2w = deal_columns(nc.scalar.copy, tile("w2w", R, U32)[:], w2w_raw, 4)
-        w2s = deal_columns(nc.vector.tensor_copy, tile("xw", R, U8)[:], w2s_raw, 16)
-
-        def vector_copy(dst, src):
-            nc.vector.tensor_copy(dst, src)
-
-        def scalar_copy(dst, src):
-            nc.scalar.activation(dst, src, COPY)
-
-        picked_a = tile("w2s_raw", PACK * O, F32)
+        picked_a = tile("w2_plane_raw", PACK * O, F32)
         picked_b = tile("picked_b", PACK * O, F32)
 
-        def first_stage(name, pair, words, scales, fmt, xwords, xscales, copy):
-            acc = ps.tile([P, 2 * J], F32, name="acc_" + name, tag="bank_" + name)
-            for u in range(2):
-                cols = slice(P * (2 * pair + u), P * (2 * pair + u + 1))
+        def first_stage(name, slices, words, plane, fmt, x, x_plane, copy):
+            count = slices.stop - slices.start
+            acc = ps.tile([P, count * J], F32, name="acc_" + name)
+            for u in range(count):
+                cols = slice(P * (slices.start + u), P * (slices.start + u + 1))
                 nc.tensor.matmul_mx(
-                    acc[:, J * u : J * (u + 1)], lhsT=words[:, cols].bitcast(fmt), lhsT_scale=scales[:, cols],
-                    rhs=xwords[:].bitcast(E4M3), rhs_scale=xscales[:], start=True, stop=True,
+                    acc[:, J * u : J * (u + 1)], lhsT=words[:, cols].bitcast(fmt), lhsT_scale=plane[:, cols],
+                    rhs=x[:].bitcast(E4M3), rhs_scale=x_plane[:], start=True, stop=True,
                 )
-            whole = tile("whole_" + name, 2 * J, F32)
+            whole = tile("whole_" + name, count * J, F32)
             copy(whole[:], acc[:])
-            return whole
-
-        def pick(whole, t, lst, picked, copy):
-            u = t % 2
-            copy(picked[:, O * t : O * (t + 1)], whole[t // 2][:, J * u : J * (u + 1)].indirect(lst[:]))
+            return [whole[:, J * u : J * (u + 1)] for u in range(count)]
 
         copies = (vector_copy, scalar_copy)
-        a = [first_stage("a%d" % pair, pair, ww, ws, E2M1, x1w, x1s, scalar_copy) for pair in range(2)]
-        b = [first_stage("b%d" % pair, pair, w2w, w2s, E5M2, x2w, x2s, copies[pair]) for pair in range(2)]
+        a, b = [], []
+        for slices in (slice(0, 1), slice(1, 2), pairs[1]):
+            a.extend(first_stage("a%d" % slices.start, slices, w, w_plane, E2M1, x1, x1_plane, scalar_copy))
+        for slices, copy in zip(pairs, copies):
+            b.extend(first_stage("b%d" % slices.start, slices, w2, w2_plane, E5M2, x2, x2_plane, copy))
+
         hid = tile("hid", PACK * O, BF16)
-        for pair in range(2):
-            for whole, lst, picked in ((a, list3, picked_a), (b, list4, picked_b)):
-                for t in (2 * pair, 2 * pair + 1):
-                    pick(whole, t, lst, picked, copies[pair])
-            slots = slice(2 * pair, 2 * pair + 2)
+        for slices, copy in zip(pairs, copies):
+            for windows, lst, picked in ((a, list3, picked_a), (b, list4, picked_b)):
+                for t in range(slices.start, slices.stop):
+                    copy(picked[:, O * t : O * (t + 1)], windows[t].indirect(lst[:]))
             nc.vector.tensor_tensor(
-                hid[:].rearrange("p (c i t) -> p c t i", t=PACK, i=4)[:, :, slots, :],
-                picked_a[:].rearrange("p (t c i) -> p c t i", t=PACK, i=4)[:, :, slots, :],
-                picked_b[:].rearrange("p (t c i) -> p c t i", t=PACK, i=4)[:, :, slots, :],
+                hid[:].rearrange("p (c i t) -> p c t i", t=PACK, i=LINE // 4)[:, :, slices, :],
+                picked_a[:].rearrange("p (t c i) -> p c t i", t=PACK, i=LINE // 4)[:, :, slices, :],
+                picked_b[:].rearrange("p (t c i) -> p c t i", t=PACK, i=LINE // 4)[:, :, slices, :],
                 MAX,
             )
-        hw = tile("hw", O, U32)
-        hs = tile("hs", O, U8)
-        nc.vector.quantize_mx(hw[:].bitcast(E4M3), hs[:], hid[:])
+        hid_words = tile("hid_words", O, U32)
+        hid_plane = tile("hid_plane", O, U8)
+        nc.vector.quantize_mx(hid_words[:].bitcast(E4M3), hid_plane[:], hid[:])
 
-        for h, (copy, queue) in enumerate(((vector_copy, nc.sync), (scalar_copy, nc.scalar))):
-            cols = slice(P * h, P * (h + 1))
-            acc = ps.tile([P, O], F32, name="acc_p%d" % h, tag="bank_p%d" % h)
+        for h, (copy, queue) in enumerate(zip(copies, (nc.sync, nc.scalar))):
+            rows = slice(P * h, P * (h + 1))
+            acc = ps.tile([P, O], F32, name="acc_p%d" % h)
             nc.tensor.matmul_mx(
-                acc[:], lhsT=wbw[:, cols].bitcast(E5M2), lhsT_scale=wbs[:, cols],
-                rhs=hw[:].bitcast(E4M3), rhs_scale=hs[:], start=True, stop=True,
+                acc[:], lhsT=wb[:, rows].bitcast(E5M2), lhsT_scale=wb_plane[:, rows],
+                rhs=hid_words[:].bitcast(E4M3), rhs_scale=hid_plane[:], start=True, stop=True,
             )
-            rows = tile("rows%d" % h, O, F32)
-            copy(rows[:], acc[:])
-            copy(pages[h][:].indirect(list5[:]), rows[:])
-            queue.dma_start(out[cols, :], pages[h][:])
+            product = tile("product%d" % h, O, F32)
+            copy(product[:], acc[:])
+            copy(pages[h][:].indirect(list5[:]), product[:])
+            queue.dma_start(out[rows, :], pages[h][:])

from contextlib import ExitStack

import concourse.mybir as mybir

K, T, J, R, O, N, E = 512, 2048, 256, 512, 128, 256, 1024
FLOPS = 2 * K * R * J * 2 + 2 * R * N * O

F32 = mybir.dt.float32
BF16 = mybir.dt.bfloat16
I32 = mybir.dt.int32
U32 = mybir.dt.uint32
U16 = mybir.dt.uint16
U8 = mybir.dt.uint8
E4M3 = mybir.dt.float8_e4m3fn_x4
E5M2 = mybir.dt.float8_e5m2_x4
E2M1 = mybir.dt.float4_e2m1fn_x4
COPY = mybir.ActivationFunctionType.Copy
MAX = mybir.AluOpType.max

P = 128
PACK = 4
QUAD = 32
LINE = 16


def tile_list_ahead_looked_one_scattered_kernel(
    tc, xt_words, xt_scales, w_words, w_scales, w2_words, w2_scales, wb_words, wb_scales,
    offs, offs2, offs3, offs4, offs5, out,
):
    nc = tc.nc
    with ExitStack() as ctx:
        sb = ctx.enter_context(tc.tile_pool(name="sb", bufs=1))
        ps = ctx.enter_context(tc.psum_pool(name="ps", bufs=1))

        def tile(buffer, cols, dtype):
            return sb.tile([P, cols], dtype, name=buffer, align_bytes=64)

        def load_list(name, src):
            lst = tile(name, src.shape[1], U16)
            nc.sync.dma_start(lst[:], src)
            return lst

        def load_words(queue, name, src, cols, dtype):
            words = tile(name, cols, dtype)
            queue.dma_start(words[:].bitcast(I32), src.bitcast(I32))
            return words

        def zeroed_plane(name, cols):
            plane = tile(name, cols, U8)
            nc.vector.memset(plane[:].bitcast(I32), 0)
            return plane

        def load_scales(queues, plane, src):
            for q, queue in enumerate(queues):
                queue.dma_start(
                    plane[QUAD * q : QUAD * q + 4, :].bitcast(I32), src[0, 4 * q : 4 * q + 4, :].bitcast(I32)
                )

        def deal_columns(move, dst, src, run, slices):
            move(
                dst[:].rearrange("p (t c i) -> p c t i", t=PACK, i=run)[:, :, slices, :],
                src[:].rearrange("p (c i t) -> p c t i", t=PACK, i=run)[:, :, slices, :],
            )

        def gather_packed(buffer, window, lst, dtype):
            picked = tile(buffer, J, dtype)
            nc.vector.tensor_copy(picked[:], window[:].indirect(lst[:]))
            return picked

        def flat(words):
            return words[0].rearrange("p n t -> p (n t)")

        def vector_copy(dst, src):
            nc.vector.tensor_copy(dst, src)

        def scalar_copy(dst, src):
            nc.scalar.activation(dst, src, COPY)

        xt_plane = tile("xt_plane", T, U8)
        nc.vector.memset(xt_plane[:, : T // 2].bitcast(I32), 0)
        nc.gpsimd.memset(xt_plane[:, T // 2 :].bitcast(I32), 0)
        w_plane_raw = zeroed_plane("w_plane_raw", R)
        w2_plane_raw = zeroed_plane("w2_plane_raw", R)
        wb_plane = zeroed_plane("wb_plane", N)
        pages = []
        for h in range(N // P):
            page = tile("page%d" % h, E, F32)
            nc.vector.memset(page[:], 0.0)
            pages.append(page)

        list1 = load_list("list1", offs)
        list2 = load_list("list2", offs2)
        w_raw = load_words(nc.scalar, "w_raw", w_words[0], R, U16)
        load_scales([nc.sync] * 2 + [nc.scalar] * 2, xt_plane, xt_scales)
        xt_table = load_words(nc.scalar, "xt_table", flat(xt_words), T, U32)
        load_scales([nc.sync] * 4, w_plane_raw, w_scales)
        w2_raw = load_words(nc.scalar, "w2_raw", flat(w2_words), R, U32)
        load_scales([nc.sync] * 4, w2_plane_raw, w2_scales)
        list3 = load_list("list3", offs3)
        list4 = load_list("list4", offs4)
        list5 = load_list("list5", offs5)
        wb = load_words(nc.sync, "wb", flat(wb_words), N, U32)
        load_scales([nc.sync] * 4, wb_plane, wb_scales)

        every = slice(0, PACK)
        pairs = [slice(0, 2), slice(2, 4)]
        x1_plane = gather_packed("x1_plane", xt_plane, list1, U8)
        w = tile("w", R, U16)
        deal_columns(nc.vector.tensor_copy, w, w_raw, LINE // 2, every)
        x2_plane = gather_packed("x2_plane", xt_plane, list2, U8)
        x1 = gather_packed("x1", xt_table, list1, U32)
        w_plane = tile("w_plane", R, U8)
        for slices in pairs:
            deal_columns(nc.vector.tensor_copy, w_plane, w_plane_raw, LINE, slices)
        x2 = gather_packed("w_plane_raw", xt_table, list2, U32)
        w2 = tile("w2", R, U32)
        deal_columns(nc.scalar.copy, w2, w2_raw, LINE // 4, every)
        w2_plane = tile("xt_table", R, U8)
        deal_columns(nc.vector.tensor_copy, w2_plane, w2_plane_raw, LINE, every)

        picked_a = tile("w2_plane_raw", PACK * O, F32)
        picked_b = tile("picked_b", PACK * O, F32)

        def first_stage(name, slices, words, plane, fmt, x, x_plane, copy):
            count = slices.stop - slices.start
            acc = ps.tile([P, count * J], F32, name="acc_" + name)
            for u in range(count):
                cols = slice(P * (slices.start + u), P * (slices.start + u + 1))
                nc.tensor.matmul_mx(
                    acc[:, J * u : J * (u + 1)], lhsT=words[:, cols].bitcast(fmt), lhsT_scale=plane[:, cols],
                    rhs=x[:].bitcast(E4M3), rhs_scale=x_plane[:], start=True, stop=True,
                )
            whole = tile("whole_" + name, count * J, F32)
            copy(whole[:], acc[:])
            return [whole[:, J * u : J * (u + 1)] for u in range(count)]

        copies = (vector_copy, scalar_copy)
        a, b = [], []
        for slices in (slice(0, 1), slice(1, 2), pairs[1]):
            a.extend(first_stage("a%d" % slices.start, slices, w, w_plane, E2M1, x1, x1_plane, scalar_copy))
        for slices, copy in zip(pairs, copies):
            b.extend(first_stage("b%d" % slices.start, slices, w2, w2_plane, E5M2, x2, x2_plane, copy))

        hid = tile("hid", PACK * O, BF16)
        for slices, copy in zip(pairs, copies):
            for windows, lst, picked in ((a, list3, picked_a), (b, list4, picked_b)):
                for t in range(slices.start, slices.stop):
                    copy(picked[:, O * t : O * (t + 1)], windows[t].indirect(lst[:]))
            nc.vector.tensor_tensor(
                hid[:].rearrange("p (c i t) -> p c t i", t=PACK, i=LINE // 4)[:, :, slices, :],
                picked_a[:].rearrange("p (t c i) -> p c t i", t=PACK, i=LINE // 4)[:, :, slices, :],
                picked_b[:].rearrange("p (t c i) -> p c t i", t=PACK, i=LINE // 4)[:, :, slices, :],
                MAX,
            )
        hid_words = tile("hid_words", O, U32)
        hid_plane = tile("hid_plane", O, U8)
        nc.vector.quantize_mx(hid_words[:].bitcast(E4M3), hid_plane[:], hid[:])

        for h, (copy, queue) in enumerate(zip(copies, (nc.sync, nc.scalar))):
            rows = slice(P * h, P * (h + 1))
            acc = ps.tile([P, O], F32, name="acc_p%d" % h)
            nc.tensor.matmul_mx(
                acc[:], lhsT=wb[:, rows].bitcast(E5M2), lhsT_scale=wb_plane[:, rows],
                rhs=hid_words[:].bitcast(E4M3), rhs_scale=hid_plane[:], start=True, stop=True,
            )
            product = tile("product%d" % h, O, F32)
            copy(product[:], acc[:])
            copy(pages[h][:].indirect(list5[:]), product[:])
            queue.dma_start(out[rows, :], pages[h][:])
